import numpy as np, ml_dtypes
CORES = [8,136,40,168]
N = 4
WB, F = 1, 64
def setup_inputs(rng):
    return {"a": rng.standard_normal((N, 128, 128), dtype=np.float32).astype(ml_dtypes.bfloat16), "w": rng.standard_normal((N, 128, F), dtype=np.float32).astype(ml_dtypes.bfloat16)}
def setup_inputs_big(rng):
    d = setup_inputs(rng)
    for k in ("a", "w"): d[k] = (d[k].astype(np.float32) * 1024.0).astype(d[k].dtype)
    return d
def setup_inputs_small(rng):
    d = setup_inputs(rng)
    for k in ("a", "w"): d[k] = (d[k].astype(np.float32) * (1 / 1024.0)).astype(d[k].dtype)
    return d
def setup_inputs_apart(rng):
    d = setup_inputs(rng)
    f = (10.0 ** rng.permutation(np.linspace(-1.5, 1.5, N))).astype(np.float32).reshape(N, 1, 1)
    for k in ("a", "w"): d[k] = (d[k].astype(np.float32) * f).astype(d[k].dtype)
    return d
def reference(a, w):
    A, W = a.astype(np.float64), w.astype(np.float64)
    p = [A[j].T @ W[j] for j in range(N)]
    y = np.stack([sum(p[r - i] for i in range(WB + 1) if r - i >= 0) for r in range(N)])
    return {"y": y.astype(ml_dtypes.bfloat16 if a.dtype != np.float64 else np.float64)}

from concourse.mybir import AluOpType

F = 64
SCRATCH = {
    "a_sb": ("sbuf", [128, 128], "bfloat16"),
    "w_sb": ("sbuf", [128, F], "bfloat16"),
    "p_ps": ("psum", [128, F], "float32"),
    "p_sb": ("sbuf", [128, F], "bfloat16"),
    "land": ("sbuf", [128, F], "bfloat16"),
    "y_sb": ("sbuf", [128, F], "bfloat16"),
}
SEMAPHORES = ["ld", "mm", "cp", "arr", "sent", "ad", "st"]

N_ENG = 8


def _engines(topo, src, dst, n):
    allowed = topo.mask(src, dst)
    bits = [b for b in range(allowed.bit_length()) if (allowed >> b) & 1]
    n = min(n, len(bits))
    m = 0
    for b in bits[:: len(bits) // n][:n]:
        m |= 1 << b
    return m, n


def rank_program(g, core, T, topo):
    r = T.rank_of(core)
    if r is None:
        return
    S = T.sem
    last = len(T.cores) - 1
    sends, receives = r < last, r > 0

    g.sync.dma_start(T.a_sb[:], T.a[:]).then_inc(S.ld, 16)
    g.scalar.dma_start(T.w_sb[:], T.w[:]).then_inc(S.ld, 16)

    g.tensor.wait_ge(S.ld, 32)
    g.tensor.matmul(T.p_ps[:], T.a_sb[:], T.w_sb[:], True, True).then_inc(S.mm, 1)

    g.vector.wait_ge(S.mm, 1)
    if sends:
        dst = T.cores[r + 1]
        assert topo.same_plane(core, dst) and topo.may_write(core, dst)
        g.vector.tensor_copy(T.p_sb[:], T.p_ps[:]).then_inc(S.cp, 1)
        rid, pid = topo.addr(dst, core)
        m, n = _engines(topo, core, dst, N_ENG)
        g.wait_ge(S.cp, 1)
        g.remote_dma(T.land[:], T.p_sb[:], S.arr, S.sent, pid, rid, m)

    if receives:
        _, n_in = _engines(topo, T.cores[r - 1], core, N_ENG)
        g.vector.wait_ge(S.arr, n_in)
        g.vector.tensor_tensor(T.y_sb[:], T.p_ps[:], T.land[:], AluOpType.add).then_inc(S.ad, 1)
        g.sync.wait_ge(S.ad, 1)
        g.sync.dma_start(T.y[:], T.y_sb[:]).then_inc(S.st, 16)
    else:
        g.sync.wait_ge(S.cp, 1)
        g.sync.dma_start(T.y[:], T.p_sb[:]).then_inc(S.st, 16)
    g.sync.wait_ge(S.st, 16)

    if sends:
        g.wait_ge(S.sent, n)
